import numpy as np
import ml_dtypes


def mxq(x, axis, fmt="e4m3"):
    dtype, down = {"e4m3": (ml_dtypes.float8_e4m3fn, 7), "e5m2": (ml_dtypes.float8_e5m2, 14)}[fmt]
    v = np.moveaxis(np.asarray(x, np.float32).astype(ml_dtypes.bfloat16).astype(np.float64), axis, -1)
    blocks = v.reshape(v.shape[:-1] + (-1, 32))
    amax = np.abs(blocks).max(-1, keepdims=True)
    byte = np.maximum(np.where(amax > 0, np.frexp(amax)[1] - 1 + 127, 0) - down, 1)
    scale = np.exp2(byte - 127.0)
    codes = (blocks / scale).astype(np.float32).astype(dtype).astype(np.float64)
    return np.moveaxis((codes * scale).reshape(v.shape), -1, axis)


WIDE = False


def mx_kscale(k):
    if not WIDE:
        return np.ones(k)
    levels = np.array([10, -10, 5, -5, 0])
    if k % 512:
        return np.exp2(np.random.permutation(np.resize(levels, k // 32))).repeat(32)
    a = np.empty((k // 512, 16))
    for p in range(k // 512):
        a[p, :8] = np.random.permutation(np.resize(levels, 8))
        for g in range(8):
            far = levels[np.abs(levels - a[p, g]) >= 10]
            a[p, g + 8] = far[np.random.randint(len(far))]
    return np.exp2(a.ravel()).repeat(32)


BF16 = ml_dtypes.bfloat16


def bf(x):
    return np.asarray(x, np.float32).astype(BF16)


def f64(x):
    return np.asarray(x).astype(np.float64)


E2M1 = np.array([0.0, 0.5, 1.0, 1.5, 2.0, 3.0, 4.0, 6.0, -0.0, -0.5, -1.0, -1.5, -2.0, -3.0, -4.0, -6.0])


def pack_weight(w, fmt):
    k, n = w.shape
    w = f64(bf(w)).reshape(k // 32, 32, n)
    amax = np.abs(w).max(1)
    if fmt == "e4m3":
        byte = np.frexp(amax)[1] - 1 + 127 - 7
    else:
        mant, ex = np.frexp(amax / 6.0)
        byte = np.where(mant > 0.5, ex, ex - 1) + 127
    byte = np.clip(np.where(amax > 0, byte, 1), 1, 254)
    scaled = (w * np.exp2(127.0 - byte)[:, None, :]).reshape(k, n).astype(np.float32)
    by_word = np.ascontiguousarray(scaled.reshape(k // 512, 128, 4, n).transpose(0, 1, 3, 2))
    if fmt == "e4m3":
        words = by_word.astype(ml_dtypes.float8_e4m3fn).view(np.uint8)
    else:
        c = by_word.astype(ml_dtypes.float4_e2m1fn).view(np.uint8) & 0xF
        words = c[..., 0::2] | (c[..., 1::2] << 4)
    return np.ascontiguousarray(words), np.ascontiguousarray(byte.astype(np.uint8).reshape(k // 512, 16, n))


def unpack_weight(words, scales, fmt):
    g, p, n, _ = words.shape
    if fmt == "e4m3":
        vals = np.ascontiguousarray(words).view(ml_dtypes.float8_e4m3fn).astype(np.float64)
    else:
        nib = np.empty((g, p, n, 4), np.uint8)
        nib[..., 0::2] = words & 0xF
        nib[..., 1::2] = words >> 4
        vals = E2M1[nib]
    vals = vals * np.repeat(np.exp2(scales.astype(np.float64) - 127.0), 8, axis=1)[..., None]
    return vals.transpose(0, 1, 3, 2).reshape(g * 512, n)
def pack4(w):
    words, scales = pack_weight(w, "e2m1")
    return words.reshape(words.shape[0], 128, -1), scales


def unpack4(words, scales):
    return unpack_weight(words.reshape(words.shape[0], 128, -1, 2), scales, "e2m1")


def planes(Y):
    n, m = Y.shape
    b = f64(bf(Y)).reshape(n // 32, 32, m)
    amax = np.abs(b).max(1)
    byte = np.clip(np.where(amax > 0, np.frexp(amax)[1] - 1 + 127 - 7, 1), 1, 254)
    codes = (b * np.exp2(127.0 - byte)[:, None, :]).reshape(n, m).astype(np.float32).astype(ml_dtypes.float8_e4m3fn).view(np.uint8)
    words = codes.reshape(n // 512, 128, 4, m).transpose(0, 1, 3, 2)
    return np.ascontiguousarray(words), np.ascontiguousarray(byte.astype(np.uint8).reshape(n // 512, 16, m))


OBS, OUTC, COMP = 2048, 512, 1024


def setup_inputs():
    rn = np.random.randn
    a = mx_kscale(OBS)
    t = mx_kscale(OUTC)
    S = rn(OBS, OBS) / np.sqrt(OBS) * a[:, None]
    s_words, s_scales = pack4(S)
    responses = bf(rn(OBS, OUTC) / a[:, None])
    gain = bf(np.exp(0.5 * rn(OUTC)) * t)
    W = np.exp(rn(OUTC, COMP)) * np.exp(0.4 * rn(COMP)) / (2.0 * OUTC) / t[:, None]
    w_words, w_scales = pack4(W)
    floor = bf(0.1 + 0.3 * np.abs(rn(COMP)))
    case_weight = bf(np.exp(0.8 * rn(OBS)))
    return dict(s_words=s_words, s_scales=s_scales, responses=responses, gain=gain,
                w_words=w_words, w_scales=w_scales, floor=floor, case_weight=case_weight)

def reference(s_words, s_scales, responses, gain, w_words, w_scales, floor, case_weight):
    S = unpack4(s_words, s_scales)
    W = unpack4(w_words, w_scales)
    R = mxq(f64(responses), 0, "e4m3")
    F = S.T @ R
    Z = F * F * f64(gain)
    V = mxq(Z, 1, "e4m3") @ W
    y = np.sqrt(V + f64(floor)) * f64(case_weight)[:, None]
    Y = y.reshape(OBS, COMP)
    words, scales = planes(Y)
    return y, words, scales

@@ -1,0 +1,373 @@
+from contextlib import ExitStack
+
+import concourse.mybir as mybir
+from concourse.masks import make_identity
+
+OBS, OUTC, COMP = 2048, 512, 1024
+FLOPS = 2 * OBS * OBS * OUTC + 2 * OBS * OUTC * COMP
+
+F32 = mybir.dt.float32
+BF16 = mybir.dt.bfloat16
+I32 = mybir.dt.int32
+U32 = mybir.dt.uint32
+U8 = mybir.dt.uint8
+FP8X4 = mybir.dt.float8_e4m3fn_x4
+FP4X4 = mybir.dt.float4_e2m1fn_x4
+ALU = mybir.AluOpType
+ACT = mybir.ActivationFunctionType
+
+P = 128
+PACK = 4
+KP = P * PACK
+GROUPS = OBS // KP
+HALF = COMP // 2
+GPSIMD_COLS = 384
+LAST_VECTOR_COLS = 344
+SQRT_MIN = 2.0 ** -116
+
+
+def tile_smoothed_square_scores_h1_kernel(
+    tc, s_words, s_scales, responses, gain, w_words, w_scales, floor, case_weight, out_0, out_1, out_2
+):
+    nc = tc.nc
+    with ExitStack() as ctx:
+        keep = ctx.enter_context(tc.tile_pool(name="keep", bufs=1))
+        work = ctx.enter_context(tc.tile_pool(name="work", bufs=2))
+        psum = ctx.enter_context(tc.psum_pool(name="psum", bufs=1))
+        ctx.enter_context(tc.manual_schedule())
+
+        def kept(name, shape, dtype):
+            return keep.tile(shape, dtype, name=name, tag=name, align_bytes=64)
+
+        def load_scale_rows(queue, plane, rows):
+            for q in range(4):
+                queue.dma_start(
+                    out=plane[32 * q : 32 * q + 4, :, :].bitcast(I32),
+                    in_=rows[:, 4 * q : 4 * q + 4, :].rearrange("g r n -> r g n").bitcast(I32),
+                )
+
+        gain_sb = kept("gain_sb", [P, PACK], BF16)
+        floor_sb = kept("floor_sb", [P, COMP // P], BF16)
+        nc.scalar.dma_start(out=gain_sb[:], in_=gain.rearrange("(p t) -> p t", t=PACK))
+        nc.scalar.dma_start(out=floor_sb[:], in_=floor.rearrange("(p c) -> p c", p=P))
+
+        s_plane_first = kept("s_plane_first", [P, GROUPS, KP], U8)
+        s_plane_second = kept("s_plane_second", [P, GROUPS, KP], U8)
+        s_plane_rest = kept("s_plane_rest", [P, GROUPS, 2 * KP], U8)
+        w_plane = kept("w_plane", [P, 1, COMP], U8)
+        for plane in (s_plane_first, s_plane_second, w_plane, s_plane_rest):
+            nc.vector.memset(plane[:].bitcast(I32), 0)
+
+        r_raw = []
+        s_first = []
+        for g in range(GROUPS):
+            raw = kept("r_raw%d" % g, [P, PACK, OUTC], BF16)
+            nc.sync.dma_start(out=raw[:], in_=responses[g * KP : (g + 1) * KP, :].rearrange("(p j) o -> p j o", j=PACK))
+            r_raw.append(raw)
+            if g == 0:
+                load_scale_rows(nc.scalar, s_plane_first, s_scales[:, :, 0:KP])
+            words = kept("s_first%d" % g, [P, 2 * KP], U8)
+            nc.sync.dma_start(out=words[:].bitcast(I32), in_=s_words[g, :, 0 : 2 * KP].bitcast(I32))
+            s_first.append(words)
+
+        def load_s_chunk(c):
+            words = kept("s_chunk%d" % c, [P, GROUPS, 2 * KP], U8)
+            nc.sync.dma_start(
+                out=words[:].bitcast(I32),
+                in_=s_words[:, :, 2 * KP * c : 2 * KP * (c + 1)].rearrange("g p n -> p g n").bitcast(I32),
+            )
+            return words
+
+        s_chunk = {1: load_s_chunk(1)}
+        load_scale_rows(nc.sync, s_plane_second, s_scales[:, :, KP : 2 * KP])
+        w_sb = kept("w_sb", [P, 2 * COMP], U8)
+        nc.sync.dma_start(out=w_sb[:].bitcast(I32), in_=w_words[0].bitcast(I32))
+        load_scale_rows(nc.sync, w_plane, w_scales)
+        cw_sb = kept("cw_sb", [P, GROUPS, PACK], BF16)
+        nc.sync.dma_start(out=cw_sb[:], in_=case_weight.rearrange("(g p t) -> p g t", p=P, t=PACK))
+        s_chunk[2] = load_s_chunk(2)
+        load_scale_rows(nc.sync, s_plane_rest, s_scales[:, :, 2 * KP :])
+        s_chunk[3] = load_s_chunk(3)
+
+        def s_operand(c, g):
+            if c == 0:
+                return s_first[g][:], s_plane_first[:, g, :]
+            if c == 1:
+                return s_chunk[c][:, g, :], s_plane_second[:, g, :]
+            return s_chunk[c][:, g, :], s_plane_rest[:, g, (c - 2) * KP : (c - 1) * KP]
+
+        ident = kept("ident", [P, P], BF16)
+        make_identity(nc, ident[:])
+        floor_ps = psum.tile([P, COMP // P, P], BF16, name="floor_ps", tag="score3")
+        for c in range(COMP // P):
+            nc.tensor.transpose(floor_ps[:, c, :], floor_sb[:, c : c + 1].to_broadcast([P, P]), ident[:])
+
+        g_neg = kept("g_neg", [P, PACK], F32)
+        g_abs = kept("g_abs", [P, PACK], F32)
+        g_guess = kept("g_guess", [P, PACK], F32)
+        g_recip = kept("g_recip", [P, PACK], F32)
+        g_corr = kept("g_corr", [P, PACK], F32)
+        g_root = kept("g_root", [P, PACK], F32)
+        g_below = kept("g_below", [P, PACK], F32)
+        g_sign = kept("g_sign", [P, PACK], F32)
+        nc.vector.tensor_scalar(out=g_neg[:], in0=gain_sb[:], scalar1=-1.0, scalar2=None, op0=ALU.mult)
+        nc.vector.tensor_scalar(out=g_below[:], in0=gain_sb[:], scalar1=0.0, scalar2=None, op0=ALU.is_lt)
+        nc.vector.scalar_tensor_tensor(
+            out=g_abs[:], in0=gain_sb[:], scalar=SQRT_MIN, in1=g_neg[:], op0=ALU.max, op1=ALU.max
+        )
+        nc.vector.scalar_tensor_tensor(
+            out=g_sign[:], in0=gain_sb[:], scalar=0.0, in1=g_below[:], op0=ALU.is_gt, op1=ALU.subtract
+        )
+        nc.scalar.activation(out=g_guess[:], in_=g_abs[:], func=ACT.Sqrt)
+        newton = [
+            lambda: nc.vector.reciprocal(out=g_recip[:], in_=g_guess[:]),
+            lambda: nc.vector.scalar_tensor_tensor(
+                out=g_corr[:], in0=g_abs[:], scalar=0.5, in1=g_recip[:], op0=ALU.mult, op1=ALU.mult
+            ),
+            lambda: nc.vector.scalar_tensor_tensor(
+                out=g_root[:], in0=g_guess[:], scalar=0.5, in1=g_corr[:], op0=ALU.mult, op1=ALU.add
+            ),
+        ]
+
+        r_codes = {}
+        r_scales = {}
+
+        def interleave_responses(g, part):
+            grouped = work.tile([P, 2, P, PACK], BF16, name="r_grouped", tag="r_grouped%d" % part, align_bytes=64)
+            dst = grouped[:].rearrange("p s (a b) j -> p a s b j", b=2)
+            src = r_raw[g][:].rearrange("p j (a b s) -> p a s b j", b=2, s=PACK)[:, :, 2 * part : 2 * part + 2, :, :]
+            if part == 0:
+                nc.vector.tensor_copy(out=dst, in_=src)
+            else:
+                nc.scalar.copy(out=dst, in_=src)
+            return grouped
+
+        def quantise_responses(g, part, grouped):
+            codes = kept("r_codes%d_%d" % (g, part), [P, 2 * P], U32)
+            scales = kept("r_scales%d_%d" % (g, part), [P, 2 * P], U8)
+            nc.vector.quantize_mx(
+                out=codes[:].bitcast(FP8X4), scales=scales[:], in_=grouped[:].rearrange("p s m j -> p (s m j)")
+            )
+            r_codes[g, part] = codes
+            r_scales[g, part] = scales
+
+        fit_ps = {}
+
+        def fit_pass(c, s, g):
+            if g == 0:
+                fit_ps[c, s] = psum.tile([P, KP], F32, name="fit_ps", tag="fit%d" % s)
+            words, plane = s_operand(c, g)
+            cols = slice((s % 2) * P, (s % 2 + 1) * P)
+            nc.tensor.matmul_mx(
+                out=fit_ps[c, s][:],
+                lhsT=r_codes[g, s // 2][:, cols].bitcast(FP8X4),
+                lhsT_scale=r_scales[g, s // 2][:, cols],
+                rhs=words.bitcast(FP4X4),
+                rhs_scale=plane,
+                start=(g == 0),
+                stop=(g == GROUPS - 1),
+            )
+
+        def fit(c, s):
+            for g in range(GROUPS):
+                fit_pass(c, s, g)
+
+        for g in range(GROUPS):
+            lower = interleave_responses(g, 0)
+            upper = interleave_responses(g, 1)
+            if g < len(newton):
+                newton[g]()
+            quantise_responses(g, 0, lower)
+            quantise_responses(g, 1, upper)
+            for s in range(PACK):
+                fit_pass(0, s, g)
+
+        floor_all = kept("floor_all", [P, COMP], F32)
+        nc.vector.tensor_copy(
+            out=floor_all[:].rearrange("p (n c) -> p n c", c=COMP // P), in_=floor_ps[:].rearrange("p c n -> p n c")
+        )
+
+        z_sq = {}
+        z_grouped = {}
+        z_codes = {}
+        z_scales = {}
+
+        def pieces(c):
+            return [(0, 2), (2, 4)] if c == 0 else [(0, 4)]
+
+        def square(c, s, piece):
+            lo, hi = piece
+            if s == 0:
+                z_sq[c, piece] = work.tile([P, PACK, (hi - lo) * P], BF16, name="z_sq", tag="z_sq", bufs=3, align_bytes=64)
+            nc.scalar.activation(
+                out=z_sq[c, piece][:, s, :].rearrange("p (u m) -> p u m", m=P),
+                in_=fit_ps[c, s][:].rearrange("p (m u) -> p u m", u=PACK)[:, lo:hi, :],
+                func=ACT.Square,
+                scale=g_root[:, s : s + 1],
+            )
+
+        def apply_sign(c, piece):
+            for s in range(PACK):
+                row = z_sq[c, piece][:, s, :]
+                nc.vector.tensor_scalar(out=row, in0=row, scalar1=g_sign[:, s : s + 1], scalar2=None, op0=ALU.mult)
+
+        def interleave_z(c, half):
+            piece = [pc for pc in pieces(c) if pc[0] <= 2 * half < pc[1]][0]
+            first = (2 * half - piece[0]) * P
+            grouped = work.tile([P, 2 * P, PACK], BF16, name="z_grouped", tag="z_grouped", align_bytes=64)
+            nc.vector.tensor_copy(
+                out=grouped[:].rearrange("p (a i) s -> p a s i", i=4),
+                in_=z_sq[c, piece][:, :, first : first + 2 * P].rearrange("p s (a i) -> p a s i", i=4),
+            )
+            z_grouped[c, half] = grouped
+
+        def quantise_z(c, half):
+            codes = work.tile([P, 2 * P], U32, name="z_codes", tag="z_codes", bufs=4, align_bytes=64)
+            scales = work.tile([P, 2 * P], U8, name="z_scales", tag="z_scales", bufs=4, align_bytes=64)
+            nc.vector.quantize_mx(
+                out=codes[:].bitcast(FP8X4), scales=scales[:], in_=z_grouped[c, half][:].rearrange("p n s -> p (n s)")
+            )
+            z_codes[c, half] = codes
+            z_scales[c, half] = scales
+
+        score_ps = {}
+        y = {}
+        y_grouped = {}
+        cw_sq = kept("cw_sq", [P, GROUPS, PACK], F32)
+        y_plane = kept("y_plane", [P, COMP], U8)
+
+        def score(c, h, u):
+            bank = psum.tile([P, HALF], F32, name="score_ps", tag="score%d" % u)
+            cols = slice((u % 2) * P, (u % 2 + 1) * P)
+            nc.tensor.matmul_mx(
+                out=bank[:],
+                lhsT=z_codes[c, u // 2][:, cols].bitcast(FP8X4),
+                lhsT_scale=z_scales[c, u // 2][:, cols],
+                rhs=w_sb[:, 2 * HALF * h : 2 * HALF * (h + 1)].bitcast(FP4X4),
+                rhs_scale=w_plane[:, 0, HALF * h : HALF * (h + 1)],
+                start=True,
+                stop=True,
+            )
+            score_ps[c, h, u] = bank
+
+        def root(c, h, u):
+            cols = slice(HALF * h, HALF * (h + 1))
+            raised = work.tile([P, HALF], F32, name="raised", tag="raised", bufs=6, align_bytes=64)
+            nc.vector.tensor_tensor(out=raised[:], in0=score_ps[c, h, u][:], in1=floor_all[:, cols], op=ALU.add)
+            if u == 0:
+                y[c, h] = work.tile([P, PACK, HALF], F32, name="y", tag="y", bufs=3, align_bytes=64)
+            nc.scalar.activation(out=y[c, h][:, u, :], in_=raised[:], func=ACT.Sqrt, scale=cw_sq[:, c, u : u + 1])
+            rows = out_0[c * KP : (c + 1) * KP, cols].rearrange("(p t) n -> p t n", t=PACK)
+            nc.sync.dma_start(out=rows[:, u, :], in_=y[c, h][:, u, :])
+
+        def grouped_tile(c, h):
+            if (c, h) not in y_grouped:
+                y_grouped[c, h] = work.tile([P, HALF, PACK], BF16, name="y_grouped", tag="y_grouped", bufs=1, align_bytes=64)
+            return y_grouped[c, h]
+
+        def round_views(c, h, lo, hi):
+            dst = grouped_tile(c, h)[:, lo:hi, :].rearrange("p (a i) t -> p a t i", i=4)
+            src = y[c, h][:, :, lo:hi].rearrange("p t (a i) -> p a t i", i=4)
+            return dst, src
+
+        def round_on_gpsimd(c, h):
+            nc.gpsimd.tensor_scalar(
+                out=grouped_tile(c, h)[:, 0:GPSIMD_COLS, :],
+                in0=y[c, h][:, :, 0:GPSIMD_COLS].rearrange("p t n -> p n t"),
+                scalar1=1.0,
+                scalar2=0.0,
+                op0=ALU.mult,
+                op1=ALU.add,
+            )
+
+        def round_on_scalar(c, h, lo):
+            dst, src = round_views(c, h, lo, HALF)
+            nc.scalar.copy(out=dst, in_=src)
+
+        def round_on_vector(c, h, hi):
+            dst, src = round_views(c, h, 0, hi)
+            nc.vector.tensor_copy(out=dst, in_=src)
+
+        def quantise_y(c, h):
+            codes = work.tile([P, HALF], U32, name="y_codes", tag="y_codes", bufs=3, align_bytes=64)
+            nc.vector.quantize_mx(
+                out=codes[:].bitcast(FP8X4),
+                scales=y_plane[PACK * c : P, HALF * h : HALF * (h + 1)],
+                in_=y_grouped[c, h][:].rearrange("p n t -> p (n t)"),
+            )
+            words = out_1[c].rearrange("p n t -> p (n t)")[:, PACK * HALF * h : PACK * HALF * (h + 1)]
+            nc.sync.dma_start(out=words.bitcast(I32), in_=codes[:].bitcast(I32))
+
+        whole = (0, PACK)
+
+        for piece in pieces(0):
+            for s in range(PACK):
+                square(0, s, piece)
+        fit(1, 0)
+        apply_sign(0, (0, 2))
+        interleave_z(0, 0)
+        nc.vector.tensor_tensor(out=cw_sq[:], in0=cw_sb[:], in1=cw_sb[:], op=ALU.mult)
+        quantise_z(0, 0)
+        score(0, 0, 0)
+        score(0, 0, 1)
+        square(1, 0, whole)
+        fit(1, 1)
+        apply_sign(0, (2, 4))
+        interleave_z(0, 1)
+        root(0, 0, 0)
+        quantise_z(0, 1)
+        score(0, 0, 2)
+        score(0, 0, 3)
+        square(1, 1, whole)
+
+        for c in range(GROUPS):
+            more = c + 1 < GROUPS
+            if c > 0:
+                round_on_gpsimd(c - 1, 1)
+                round_on_scalar(c - 1, 1, GPSIMD_COLS)
+                for u in range(PACK):
+                    score(c, 0, u)
+            if more:
+                fit(c + 1, 2)
+            for u in range(1 if c == 0 else 0, PACK):
+                root(c, 0, u)
+            if c > 0:
+                quantise_y(c - 1, 1)
+            for u in range(PACK):
+                score(c, 1, u)
+            round_on_gpsimd(c, 0)
+            if more:
+                square(c + 1, 2, whole)
+                fit(c + 1, 3)
+            else:
+                round_on_scalar(c, 0, GPSIMD_COLS)
+            root(c, 1, 0)
+            root(c, 1, 1)
+            if more:
+                square(c + 1, 3, whole)
+            root(c, 1, 2)
+            root(c, 1, 3)
+            if c + 2 < GROUPS:
+                fit(c + 2, 0)
+                fit(c + 2, 1)
+            if more:
+                round_on_scalar(c, 0, GPSIMD_COLS)
+                apply_sign(c + 1, whole)
+                for half in range(2):
+                    interleave_z(c + 1, half)
+                for half in range(2):
+                    quantise_z(c + 1, half)
+            quantise_y(c, 0)
+            if c + 2 < GROUPS:
+                square(c + 2, 0, whole)
+                square(c + 2, 1, whole)
+
+        last = GROUPS - 1
+        round_on_vector(last, 1, LAST_VECTOR_COLS)
+        round_on_scalar(last, 1, LAST_VECTOR_COLS)
+        quantise_y(last, 1)
+        for q in range(4):
+            nc.scalar.dma_start(
+                out=out_2[:, 4 * q : 4 * q + 4, :].bitcast(I32),
+                in_=y_plane[32 * q : 32 * q + 16, :].bitcast(I32),
+            )

@@ -21,8 +21,7 @@ PACK = 4
 KP = P * PACK
 GROUPS = OBS // KP
 HALF = COMP // 2
-GPSIMD_COLS = 384
-LAST_VECTOR_COLS = 344
+LAST_VECTOR_COLS = 192
 SQRT_MIN = 2.0 ** -116
 
 
@@ -236,69 +235,67 @@ def tile_smoothed_square_scores_h1_kernel(
         cw_sq = kept("cw_sq", [P, GROUPS, PACK], F32)
         y_plane = kept("y_plane", [P, COMP], U8)
 
-        def score(c, h, u):
-            bank = psum.tile([P, HALF], F32, name="score_ps", tag="score%d" % u)
+        def score(unit, u):
+            c, lo, hi = unit
+            bank = psum.tile([P, hi - lo], F32, name="score_ps", tag="score%d" % u)
             cols = slice((u % 2) * P, (u % 2 + 1) * P)
             nc.tensor.matmul_mx(
                 out=bank[:],
                 lhsT=z_codes[c, u // 2][:, cols].bitcast(FP8X4),
                 lhsT_scale=z_scales[c, u // 2][:, cols],
-                rhs=w_sb[:, 2 * HALF * h : 2 * HALF * (h + 1)].bitcast(FP4X4),
-                rhs_scale=w_plane[:, 0, HALF * h : HALF * (h + 1)],
+                rhs=w_sb[:, 2 * lo : 2 * hi].bitcast(FP4X4),
+                rhs_scale=w_plane[:, 0, lo:hi],
                 start=True,
                 stop=True,
             )
-            score_ps[c, h, u] = bank
+            score_ps[unit, u] = bank
 
-        def root(c, h, u):
-            cols = slice(HALF * h, HALF * (h + 1))
-            raised = work.tile([P, HALF], F32, name="raised", tag="raised", bufs=6, align_bytes=64)
-            nc.vector.tensor_tensor(out=raised[:], in0=score_ps[c, h, u][:], in1=floor_all[:, cols], op=ALU.add)
+        def root(unit, u):
+            c, lo, hi = unit
+            raised = work.tile([P, hi - lo], F32, name="raised", tag="raised", bufs=6, align_bytes=64)
+            nc.vector.tensor_tensor(out=raised[:], in0=score_ps[unit, u][:], in1=floor_all[:, lo:hi], op=ALU.add)
             if u == 0:
-                y[c, h] = work.tile([P, PACK, HALF], F32, name="y", tag="y", bufs=3, align_bytes=64)
-            nc.scalar.activation(out=y[c, h][:, u, :], in_=raised[:], func=ACT.Sqrt, scale=cw_sq[:, c, u : u + 1])
-            rows = out_0[c * KP : (c + 1) * KP, cols].rearrange("(p t) n -> p t n", t=PACK)
-            nc.sync.dma_start(out=rows[:, u, :], in_=y[c, h][:, u, :])
+                y[unit] = work.tile([P, PACK, hi - lo], F32, name="y", tag="y", bufs=3, align_bytes=64)
+            nc.scalar.activation(out=y[unit][:, u, :], in_=raised[:], func=ACT.Sqrt, scale=cw_sq[:, c, u : u + 1])
+            rows = out_0[c * KP : (c + 1) * KP, lo:hi].rearrange("(p t) n -> p t n", t=PACK)
+            nc.sync.dma_start(out=rows[:, u, :], in_=y[unit][:, u, :])
 
-        def grouped_tile(c, h):
-            if (c, h) not in y_grouped:
-                y_grouped[c, h] = work.tile([P, HALF, PACK], BF16, name="y_grouped", tag="y_grouped", bufs=1, align_bytes=64)
-            return y_grouped[c, h]
-
-        def round_views(c, h, lo, hi):
-            dst = grouped_tile(c, h)[:, lo:hi, :].rearrange("p (a i) t -> p a t i", i=4)
-            src = y[c, h][:, :, lo:hi].rearrange("p t (a i) -> p a t i", i=4)
+        def round_views(unit, first, end):
+            if unit not in y_grouped:
+                y_grouped[unit] = work.tile(
+                    [P, unit[2] - unit[1], PACK], BF16, name="y_grouped", tag="y_grouped", align_bytes=64
+                )
+            dst = y_grouped[unit][:, first:end, :].rearrange("p (a i) t -> p a t i", i=4)
+            src = y[unit][:, :, first:end].rearrange("p t (a i) -> p a t i", i=4)
             return dst, src
 
-        def round_on_gpsimd(c, h):
-            nc.gpsimd.tensor_scalar(
-                out=grouped_tile(c, h)[:, 0:GPSIMD_COLS, :],
-                in0=y[c, h][:, :, 0:GPSIMD_COLS].rearrange("p t n -> p n t"),
-                scalar1=1.0,
-                scalar2=0.0,
-                op0=ALU.mult,
-                op1=ALU.add,
-            )
+        def vector_cols(unit):
+            width = unit[2] - unit[1]
+            return LAST_VECTOR_COLS if unit == units[-1] else width // 2
 
-        def round_on_scalar(c, h, lo):
-            dst, src = round_views(c, h, lo, HALF)
-            nc.scalar.copy(out=dst, in_=src)
-
-        def round_on_vector(c, h, hi):
-            dst, src = round_views(c, h, 0, hi)
+        def round_on_vector(unit):
+            dst, src = round_views(unit, 0, vector_cols(unit))
             nc.vector.tensor_copy(out=dst, in_=src)
 
-        def quantise_y(c, h):
-            codes = work.tile([P, HALF], U32, name="y_codes", tag="y_codes", bufs=3, align_bytes=64)
+        def round_on_scalar(unit):
+            dst, src = round_views(unit, vector_cols(unit), unit[2] - unit[1])
+            nc.scalar.copy(out=dst, in_=src)
+
+        def quantise_y(unit):
+            c, lo, hi = unit
+            codes = work.tile([P, hi - lo], U32, name="y_codes", tag="y_codes", bufs=3, align_bytes=64)
             nc.vector.quantize_mx(
                 out=codes[:].bitcast(FP8X4),
-                scales=y_plane[PACK * c : P, HALF * h : HALF * (h + 1)],
-                in_=y_grouped[c, h][:].rearrange("p n t -> p (n t)"),
+                scales=y_plane[PACK * c : P, lo:hi],
+                in_=y_grouped[unit][:].rearrange("p n t -> p (n t)"),
             )
-            words = out_1[c].rearrange("p n t -> p (n t)")[:, PACK * HALF * h : PACK * HALF * (h + 1)]
+            words = out_1[c].rearrange("p n t -> p (n t)")[:, PACK * lo : PACK * hi]
             nc.sync.dma_start(out=words.bitcast(I32), in_=codes[:].bitcast(I32))
 
         whole = (0, PACK)
+        last = GROUPS - 1
+        units = [(c, HALF * h, HALF * (h + 1)) for c in range(GROUPS) for h in range(2)][:-1]
+        units = units + [(last, HALF, HALF + HALF // 2), (last, HALF + HALF // 2, COMP)]
 
         for piece in pieces(0):
             for s in range(PACK):
@@ -308,64 +305,77 @@ def tile_smoothed_square_scores_h1_kernel(
         interleave_z(0, 0)
         nc.vector.tensor_tensor(out=cw_sq[:], in0=cw_sb[:], in1=cw_sb[:], op=ALU.mult)
         quantise_z(0, 0)
-        score(0, 0, 0)
-        score(0, 0, 1)
+        score(units[0], 0)
+        score(units[0], 1)
         square(1, 0, whole)
         fit(1, 1)
         apply_sign(0, (2, 4))
         interleave_z(0, 1)
-        root(0, 0, 0)
+        root(units[0], 0)
         quantise_z(0, 1)
-        score(0, 0, 2)
-        score(0, 0, 3)
+        score(units[0], 2)
+        score(units[0], 3)
         square(1, 1, whole)
 
         for c in range(GROUPS):
             more = c + 1 < GROUPS
+            left, right = units[2 * c], units[2 * c + 1]
             if c > 0:
-                round_on_gpsimd(c - 1, 1)
-                round_on_scalar(c - 1, 1, GPSIMD_COLS)
+                before = units[2 * c - 1]
+                round_on_scalar(before)
                 for u in range(PACK):
-                    score(c, 0, u)
+                    score(left, u)
             if more:
                 fit(c + 1, 2)
             for u in range(1 if c == 0 else 0, PACK):
-                root(c, 0, u)
+                root(left, u)
             if c > 0:
-                quantise_y(c - 1, 1)
+                round_on_vector(before)
             for u in range(PACK):
-                score(c, 1, u)
-            round_on_gpsimd(c, 0)
+                score(right, u)
             if more:
                 square(c + 1, 2, whole)
                 fit(c + 1, 3)
             else:
-                round_on_scalar(c, 0, GPSIMD_COLS)
-            root(c, 1, 0)
-            root(c, 1, 1)
+                round_on_scalar(left)
+            root(right, 0)
+            if c > 0:
+                quantise_y(before)
+            root(right, 1)
             if more:
                 square(c + 1, 3, whole)
-            root(c, 1, 2)
-            root(c, 1, 3)
+            root(right, 2)
+            root(right, 3)
             if c + 2 < GROUPS:
                 fit(c + 2, 0)
                 fit(c + 2, 1)
             if more:
-                round_on_scalar(c, 0, GPSIMD_COLS)
+                round_on_scalar(left)
                 apply_sign(c + 1, whole)
+                round_on_vector(left)
                 for half in range(2):
                     interleave_z(c + 1, half)
                 for half in range(2):
                     quantise_z(c + 1, half)
-            quantise_y(c, 0)
+                quantise_y(left)
             if c + 2 < GROUPS:
                 square(c + 2, 0, whole)
                 square(c + 2, 1, whole)
 
-        last = GROUPS - 1
-        round_on_vector(last, 1, LAST_VECTOR_COLS)
-        round_on_scalar(last, 1, LAST_VECTOR_COLS)
-        quantise_y(last, 1)
+        left, right, final = units[-3:]
+        for u in range(PACK):
+            score(final, u)
+        round_on_vector(left)
+        root(final, 0)
+        quantise_y(left)
+        for u in range(1, PACK):
+            root(final, u)
+        round_on_vector(right)
+        round_on_scalar(right)
+        round_on_vector(final)
+        round_on_scalar(final)
+        quantise_y(right)
+        quantise_y(final)
         for q in range(4):
             nc.scalar.dma_start(
                 out=out_2[:, 4 * q : 4 * q + 4, :].bitcast(I32),

@@ -21,7 +21,8 @@ PACK = 4
 KP = P * PACK
 GROUPS = OBS // KP
 HALF = COMP // 2
-LAST_VECTOR_COLS = 192
+GPSIMD_COLS = 288
+TAIL_VECTOR_COLS = (96, 128)
 SQRT_MIN = 2.0 ** -116
 
 
@@ -48,58 +49,56 @@ def tile_smoothed_square_scores_h1_kernel(
         gain_sb = kept("gain_sb", [P, PACK], BF16)
         floor_sb = kept("floor_sb", [P, COMP // P], BF16)
         nc.scalar.dma_start(out=gain_sb[:], in_=gain.rearrange("(p t) -> p t", t=PACK))
-        nc.scalar.dma_start(out=floor_sb[:], in_=floor.rearrange("(p c) -> p c", p=P))
+        nc.gpsimd.dma_start(out=floor_sb[:], in_=floor.rearrange("(p c) -> p c", p=P))
 
-        s_plane_first = kept("s_plane_first", [P, GROUPS, KP], U8)
-        s_plane_second = kept("s_plane_second", [P, GROUPS, KP], U8)
-        s_plane_rest = kept("s_plane_rest", [P, GROUPS, 2 * KP], U8)
+        cw_sb = kept("cw_sb", [P, GROUPS, 16], BF16)
+        nc.gpsimd.dma_start(out=cw_sb[:, :, 0:PACK], in_=case_weight.rearrange("(g p t) -> p g t", p=P, t=PACK))
+
+        s_plane = [kept("s_plane%d" % i, [P, GROUPS, 2 * KP], U8) for i in range(2)]
         w_plane = kept("w_plane", [P, 1, COMP], U8)
-        for plane in (s_plane_first, s_plane_second, w_plane, s_plane_rest):
+        for plane in (s_plane[0], w_plane, s_plane[1]):
             nc.vector.memset(plane[:].bitcast(I32), 0)
 
-        r_raw = []
-        s_first = []
-        for g in range(GROUPS):
-            raw = kept("r_raw%d" % g, [P, PACK, OUTC], BF16)
-            nc.sync.dma_start(out=raw[:], in_=responses[g * KP : (g + 1) * KP, :].rearrange("(p j) o -> p j o", j=PACK))
-            r_raw.append(raw)
-            if g == 0:
-                load_scale_rows(nc.scalar, s_plane_first, s_scales[:, :, 0:KP])
-            words = kept("s_first%d" % g, [P, 2 * KP], U8)
-            nc.sync.dma_start(out=words[:].bitcast(I32), in_=s_words[g, :, 0 : 2 * KP].bitcast(I32))
-            s_first.append(words)
+        r_raw = {}
+        s_sb = {}
 
-        def load_s_chunk(c):
-            words = kept("s_chunk%d" % c, [P, GROUPS, 2 * KP], U8)
+        def load_responses(g):
+            r_raw[g] = kept("r_raw%d" % g, [P, PACK, OUTC], BF16)
+            nc.sync.dma_start(
+                out=r_raw[g][:], in_=responses[g * KP : (g + 1) * KP, :].rearrange("(p j) o -> p j o", j=PACK)
+            )
+
+        def load_s(c, first, end):
+            words = kept("s_sb%d_%d" % (c, first), [P, end - first, 2 * KP], U8)
             nc.sync.dma_start(
                 out=words[:].bitcast(I32),
-                in_=s_words[:, :, 2 * KP * c : 2 * KP * (c + 1)].rearrange("g p n -> p g n").bitcast(I32),
+                in_=s_words[first:end, :, 2 * KP * c : 2 * KP * (c + 1)].rearrange("g p n -> p g n").bitcast(I32),
             )
-            return words
+            for g in range(first, end):
+                s_sb[c, g] = words[:, g - first, :]
 
-        s_chunk = {1: load_s_chunk(1)}
-        load_scale_rows(nc.sync, s_plane_second, s_scales[:, :, KP : 2 * KP])
+        load_responses(0)
+        load_scale_rows(nc.sync, s_plane[0], s_scales[:, :, 0 : 2 * KP])
+        load_s(0, 0, 2)
+        load_responses(1)
+        load_responses(2)
+        load_s(0, 2, 3)
+        load_responses(3)
+        load_s(0, 3, 4)
         w_sb = kept("w_sb", [P, 2 * COMP], U8)
         nc.sync.dma_start(out=w_sb[:].bitcast(I32), in_=w_words[0].bitcast(I32))
         load_scale_rows(nc.sync, w_plane, w_scales)
-        cw_sb = kept("cw_sb", [P, GROUPS, PACK], BF16)
-        nc.sync.dma_start(out=cw_sb[:], in_=case_weight.rearrange("(g p t) -> p g t", p=P, t=PACK))
-        s_chunk[2] = load_s_chunk(2)
-        load_scale_rows(nc.sync, s_plane_rest, s_scales[:, :, 2 * KP :])
-        s_chunk[3] = load_s_chunk(3)
+        load_s(1, 0, GROUPS)
+        load_s(2, 0, GROUPS)
+        load_scale_rows(nc.sync, s_plane[1], s_scales[:, :, 2 * KP :])
+        load_s(3, 0, GROUPS)
 
         def s_operand(c, g):
-            if c == 0:
-                return s_first[g][:], s_plane_first[:, g, :]
-            if c == 1:
-                return s_chunk[c][:, g, :], s_plane_second[:, g, :]
-            return s_chunk[c][:, g, :], s_plane_rest[:, g, (c - 2) * KP : (c - 1) * KP]
+            return s_sb[c, g], s_plane[c // 2][:, g, (c % 2) * KP : (c % 2 + 1) * KP]
 
         ident = kept("ident", [P, P], BF16)
         make_identity(nc, ident[:])
         floor_ps = psum.tile([P, COMP // P, P], BF16, name="floor_ps", tag="score3")
-        for c in range(COMP // P):
-            nc.tensor.transpose(floor_ps[:, c, :], floor_sb[:, c : c + 1].to_broadcast([P, P]), ident[:])
 
         g_neg = kept("g_neg", [P, PACK], F32)
         g_abs = kept("g_abs", [P, PACK], F32)
@@ -118,6 +117,7 @@ def tile_smoothed_square_scores_h1_kernel(
             out=g_sign[:], in0=gain_sb[:], scalar=0.0, in1=g_below[:], op0=ALU.is_gt, op1=ALU.subtract
         )
         nc.scalar.activation(out=g_guess[:], in_=g_abs[:], func=ACT.Sqrt)
+        cw_sq = kept("cw_sq", [P, GROUPS, PACK], F32)
         newton = [
             lambda: nc.vector.reciprocal(out=g_recip[:], in_=g_guess[:]),
             lambda: nc.vector.scalar_tensor_tensor(
@@ -126,6 +126,7 @@ def tile_smoothed_square_scores_h1_kernel(
             lambda: nc.vector.scalar_tensor_tensor(
                 out=g_root[:], in0=g_guess[:], scalar=0.5, in1=g_corr[:], op0=ALU.mult, op1=ALU.add
             ),
+            lambda: nc.vector.tensor_tensor(out=cw_sq[:], in0=cw_sb[:, :, 0:PACK], in1=cw_sb[:, :, 0:PACK], op=ALU.mult),
         ]
 
         r_codes = {}
@@ -171,20 +172,37 @@ def tile_smoothed_square_scores_h1_kernel(
             for g in range(GROUPS):
                 fit_pass(c, s, g)
 
-        for g in range(GROUPS):
-            lower = interleave_responses(g, 0)
-            upper = interleave_responses(g, 1)
-            if g < len(newton):
-                newton[g]()
-            quantise_responses(g, 0, lower)
-            quantise_responses(g, 1, upper)
-            for s in range(PACK):
-                fit_pass(0, s, g)
+        def spread_floor():
+            for c in range(COMP // P):
+                nc.tensor.transpose(floor_ps[:, c, :], floor_sb[:, c : c + 1].to_broadcast([P, P]), ident[:])
 
-        floor_all = kept("floor_all", [P, COMP], F32)
-        nc.vector.tensor_copy(
-            out=floor_all[:].rearrange("p (n c) -> p n c", c=COMP // P), in_=floor_ps[:].rearrange("p c n -> p n c")
-        )
+        upper = {}
+        for g in range(GROUPS + 1):
+            if g < GROUPS:
+                lower = interleave_responses(g, 0)
+                upper[g] = interleave_responses(g, 1)
+                newton[g]()
+            if g > 0:
+                quantise_responses(g - 1, 1, upper[g - 1])
+                fit_pass(0, 2, g - 1)
+                fit_pass(0, 3, g - 1)
+            if g == 1:
+                spread_floor()
+            if g < GROUPS:
+                quantise_responses(g, 0, lower)
+                fit_pass(0, 0, g)
+                fit_pass(0, 1, g)
+
+        floor_all = [kept("floor_all%d" % h, [P, HALF], F32) for h in range(2)]
+
+        def copy_floor(h):
+            nc.scalar.copy(
+                out=floor_all[h][:].rearrange("p (n c) -> p n c", c=COMP // P),
+                in_=floor_ps[:, :, h * P // 2 : (h + 1) * P // 2].rearrange("p c n -> p n c"),
+            )
+
+        copy_floor(0)
+        copy_floor(1)
 
         z_sq = {}
         z_grouped = {}
@@ -205,8 +223,8 @@ def tile_smoothed_square_scores_h1_kernel(
                 scale=g_root[:, s : s + 1],
             )
 
-        def apply_sign(c, piece):
-            for s in range(PACK):
+        def apply_sign(c, piece, slots):
+            for s in slots:
                 row = z_sq[c, piece][:, s, :]
                 nc.vector.tensor_scalar(out=row, in0=row, scalar1=g_sign[:, s : s + 1], scalar2=None, op0=ALU.mult)
 
@@ -232,7 +250,6 @@ def tile_smoothed_square_scores_h1_kernel(
         score_ps = {}
         y = {}
         y_grouped = {}
-        cw_sq = kept("cw_sq", [P, GROUPS, PACK], F32)
         y_plane = kept("y_plane", [P, COMP], U8)
 
         def score(unit, u):
@@ -253,44 +270,65 @@ def tile_smoothed_square_scores_h1_kernel(
         def root(unit, u):
             c, lo, hi = unit
             raised = work.tile([P, hi - lo], F32, name="raised", tag="raised", bufs=6, align_bytes=64)
-            nc.vector.tensor_tensor(out=raised[:], in0=score_ps[unit, u][:], in1=floor_all[:, lo:hi], op=ALU.add)
+            nc.vector.tensor_tensor(out=raised[:], in0=score_ps[unit, u][:], in1=floor_all[lo // HALF][:, lo % HALF : lo % HALF + hi - lo], op=ALU.add)
             if u == 0:
                 y[unit] = work.tile([P, PACK, hi - lo], F32, name="y", tag="y", bufs=3, align_bytes=64)
             nc.scalar.activation(out=y[unit][:, u, :], in_=raised[:], func=ACT.Sqrt, scale=cw_sq[:, c, u : u + 1])
-            rows = out_0[c * KP : (c + 1) * KP, lo:hi].rearrange("(p t) n -> p t n", t=PACK)
-            nc.sync.dma_start(out=rows[:, u, :], in_=y[unit][:, u, :])
+            run = PACK if unit in units[-2:] else 2
+            if (u + 1) % run == 0:
+                rows = out_0[c * KP : (c + 1) * KP, lo:hi].rearrange("(p t) n -> p t n", t=PACK)
+                nc.sync.dma_start(out=rows[:, u + 1 - run : u + 1, :], in_=y[unit][:, u + 1 - run : u + 1, :])
+
+        shared = kept("y_shared", [P, 2 * HALF - GPSIMD_COLS, PACK], BF16)
+
+        def grouped_view(unit):
+            if unit in units[-2:]:
+                if unit not in y_grouped:
+                    y_grouped[unit] = work.tile([P, HALF // 2, PACK], BF16, name="y_tail", tag="y_tail", align_bytes=64)
+                return y_grouped[unit][:]
+            start = 0 if unit[1] == 0 else HALF - GPSIMD_COLS
+            return shared[:, start : start + HALF, :]
 
         def round_views(unit, first, end):
-            if unit not in y_grouped:
-                y_grouped[unit] = work.tile(
-                    [P, unit[2] - unit[1], PACK], BF16, name="y_grouped", tag="y_grouped", align_bytes=64
-                )
-            dst = y_grouped[unit][:, first:end, :].rearrange("p (a i) t -> p a t i", i=4)
+            dst = grouped_view(unit)[:, first:end, :].rearrange("p (a i) t -> p a t i", i=4)
             src = y[unit][:, :, first:end].rearrange("p t (a i) -> p a t i", i=4)
             return dst, src
 
-        def vector_cols(unit):
-            width = unit[2] - unit[1]
-            return LAST_VECTOR_COLS if unit == units[-1] else width // 2
+        def round_on_gpsimd(unit):
+            first = HALF - GPSIMD_COLS if unit[1] == 0 else 0
+            nc.gpsimd.tensor_scalar(
+                out=grouped_view(unit)[:, first : first + GPSIMD_COLS, :],
+                in0=y[unit][:, :, first : first + GPSIMD_COLS].rearrange("p t n -> p n t"),
+                scalar1=1.0,
+                scalar2=0.0,
+                op0=ALU.mult,
+                op1=ALU.add,
+            )
 
-        def round_on_vector(unit):
-            dst, src = round_views(unit, 0, vector_cols(unit))
+        def round_on_vector(unit, end):
+            dst, src = round_views(unit, 0, end)
             nc.vector.tensor_copy(out=dst, in_=src)
 
-        def round_on_scalar(unit):
-            dst, src = round_views(unit, vector_cols(unit), unit[2] - unit[1])
+        def round_on_scalar(unit, first, end):
+            dst, src = round_views(unit, first, end)
             nc.scalar.copy(out=dst, in_=src)
+
+        y_codes = {}
 
         def quantise_y(unit):
             c, lo, hi = unit
-            codes = work.tile([P, hi - lo], U32, name="y_codes", tag="y_codes", bufs=3, align_bytes=64)
+            start = lo - lo % HALF
+            if lo == start:
+                y_codes[c, start] = work.tile([P, HALF], U32, name="y_codes", tag="y_codes", bufs=3, align_bytes=64)
+            codes = y_codes[c, start]
             nc.vector.quantize_mx(
-                out=codes[:].bitcast(FP8X4),
+                out=codes[:, lo - start : hi - start].bitcast(FP8X4),
                 scales=y_plane[PACK * c : P, lo:hi],
-                in_=y_grouped[unit][:].rearrange("p n t -> p (n t)"),
+                in_=grouped_view(unit).rearrange("p n t -> p (n t)"),
             )
-            words = out_1[c].rearrange("p n t -> p (n t)")[:, PACK * lo : PACK * hi]
-            nc.sync.dma_start(out=words.bitcast(I32), in_=codes[:].bitcast(I32))
+            if hi == start + HALF:
+                words = out_1[c].rearrange("p n t -> p (n t)")[:, PACK * start : PACK * hi]
+                nc.sync.dma_start(out=words.bitcast(I32), in_=codes[:].bitcast(I32))
 
         whole = (0, PACK)
         last = GROUPS - 1
@@ -301,15 +339,15 @@ def tile_smoothed_square_scores_h1_kernel(
             for s in range(PACK):
                 square(0, s, piece)
         fit(1, 0)
-        apply_sign(0, (0, 2))
+        apply_sign(0, (0, 2), range(PACK))
         interleave_z(0, 0)
-        nc.vector.tensor_tensor(out=cw_sq[:], in0=cw_sb[:], in1=cw_sb[:], op=ALU.mult)
+        apply_sign(0, (2, 4), range(PACK - 1))
         quantise_z(0, 0)
         score(units[0], 0)
         score(units[0], 1)
         square(1, 0, whole)
         fit(1, 1)
-        apply_sign(0, (2, 4))
+        apply_sign(0, (2, 4), [PACK - 1])
         interleave_z(0, 1)
         root(units[0], 0)
         quantise_z(0, 1)
@@ -322,25 +360,24 @@ def tile_smoothed_square_scores_h1_kernel(
             left, right = units[2 * c], units[2 * c + 1]
             if c > 0:
                 before = units[2 * c - 1]
-                round_on_scalar(before)
+                round_on_gpsimd(before)
                 for u in range(PACK):
                     score(left, u)
-            if more:
+            if more and c > 0:
                 fit(c + 1, 2)
             for u in range(1 if c == 0 else 0, PACK):
                 root(left, u)
             if c > 0:
-                round_on_vector(before)
+                quantise_y(before)
             for u in range(PACK):
                 score(right, u)
+                if c == 0 and u == 1:
+                    fit(1, 2)
+            round_on_gpsimd(left)
             if more:
                 square(c + 1, 2, whole)
                 fit(c + 1, 3)
-            else:
-                round_on_scalar(left)
             root(right, 0)
-            if c > 0:
-                quantise_y(before)
             root(right, 1)
             if more:
                 square(c + 1, 3, whole)
@@ -350,9 +387,9 @@ def tile_smoothed_square_scores_h1_kernel(
                 fit(c + 2, 0)
                 fit(c + 2, 1)
             if more:
-                round_on_scalar(left)
-                apply_sign(c + 1, whole)
-                round_on_vector(left)
+                round_on_scalar(left, 0, HALF - GPSIMD_COLS)
+                round_on_scalar(right, GPSIMD_COLS, HALF)
+                apply_sign(c + 1, whole, range(PACK))
                 for half in range(2):
                     interleave_z(c + 1, half)
                 for half in range(2):
@@ -365,15 +402,13 @@ def tile_smoothed_square_scores_h1_kernel(
         left, right, final = units[-3:]
         for u in range(PACK):
             score(final, u)
-        round_on_vector(left)
-        root(final, 0)
-        quantise_y(left)
-        for u in range(1, PACK):
             root(final, u)
-        round_on_vector(right)
-        round_on_scalar(right)
-        round_on_vector(final)
-        round_on_scalar(final)
+        round_on_vector(left, HALF - GPSIMD_COLS)
+        for unit, cols in zip((right, final), TAIL_VECTOR_COLS):
+            round_on_vector(unit, cols)
+            round_on_scalar(unit, cols, HALF // 2)
+            if unit == right:
+                quantise_y(left)
         quantise_y(right)
         quantise_y(final)
         for q in range(4):

@@ -22,7 +22,9 @@ KP = P * PACK
 GROUPS = OBS // KP
 HALF = COMP // 2
 GPSIMD_COLS = 288
-TAIL_VECTOR_COLS = (96, 128)
+LEFT_VECTOR_COLS = 112
+RIGHT_VECTOR_COLS = 0
+TAIL_VECTOR_COLS = (128, 160)
 SQRT_MIN = 2.0 ** -116
 
 
@@ -172,26 +174,28 @@ def tile_smoothed_square_scores_h1_kernel(
             for g in range(GROUPS):
                 fit_pass(c, s, g)
 
-        def spread_floor():
-            for c in range(COMP // P):
-                nc.tensor.transpose(floor_ps[:, c, :], floor_sb[:, c : c + 1].to_broadcast([P, P]), ident[:])
+        def finish_upper(g, grouped):
+            quantise_responses(g, 1, grouped)
+            fit_pass(0, 2, g)
+            fit_pass(0, 3, g)
 
-        upper = {}
-        for g in range(GROUPS + 1):
-            if g < GROUPS:
-                lower = interleave_responses(g, 0)
-                upper[g] = interleave_responses(g, 1)
-                newton[g]()
-            if g > 0:
-                quantise_responses(g - 1, 1, upper[g - 1])
-                fit_pass(0, 2, g - 1)
-                fit_pass(0, 3, g - 1)
-            if g == 1:
-                spread_floor()
-            if g < GROUPS:
-                quantise_responses(g, 0, lower)
-                fit_pass(0, 0, g)
-                fit_pass(0, 1, g)
+        waiting = None
+        for g in range(GROUPS):
+            lower = interleave_responses(g, 0)
+            upper = interleave_responses(g, 1)
+            newton[g]()
+            if waiting is not None:
+                finish_upper(g - 1, waiting)
+            quantise_responses(g, 0, lower)
+            fit_pass(0, 0, g)
+            fit_pass(0, 1, g)
+            waiting = upper
+            if g in (0, GROUPS - 1):
+                finish_upper(g, upper)
+                waiting = None
+
+        for c in range(COMP // P):
+            nc.tensor.transpose(floor_ps[:, c, :], floor_sb[:, c : c + 1].to_broadcast([P, P]), ident[:])
 
         floor_all = [kept("floor_all%d" % h, [P, HALF], F32) for h in range(2)]
 
@@ -200,9 +204,6 @@ def tile_smoothed_square_scores_h1_kernel(
                 out=floor_all[h][:].rearrange("p (n c) -> p n c", c=COMP // P),
                 in_=floor_ps[:, :, h * P // 2 : (h + 1) * P // 2].rearrange("p c n -> p n c"),
             )
-
-        copy_floor(0)
-        copy_floor(1)
 
         z_sq = {}
         z_grouped = {}
@@ -305,13 +306,15 @@ def tile_smoothed_square_scores_h1_kernel(
                 op1=ALU.add,
             )
 
-        def round_on_vector(unit, end):
-            dst, src = round_views(unit, 0, end)
-            nc.vector.tensor_copy(out=dst, in_=src)
+        def round_on_vector(unit, first, end):
+            if end > first:
+                dst, src = round_views(unit, first, end)
+                nc.vector.tensor_copy(out=dst, in_=src)
 
         def round_on_scalar(unit, first, end):
-            dst, src = round_views(unit, first, end)
-            nc.scalar.copy(out=dst, in_=src)
+            nc.scalar.copy(
+                out=grouped_view(unit)[:, first:end, :], in_=y[unit][:, :, first:end].rearrange("p t n -> p n t")
+            )
 
         y_codes = {}
 
@@ -338,6 +341,7 @@ def tile_smoothed_square_scores_h1_kernel(
         for piece in pieces(0):
             for s in range(PACK):
                 square(0, s, piece)
+        copy_floor(0)
         fit(1, 0)
         apply_sign(0, (0, 2), range(PACK))
         interleave_z(0, 0)
@@ -346,6 +350,7 @@ def tile_smoothed_square_scores_h1_kernel(
         score(units[0], 0)
         score(units[0], 1)
         square(1, 0, whole)
+        copy_floor(1)
         fit(1, 1)
         apply_sign(0, (2, 4), [PACK - 1])
         interleave_z(0, 1)
@@ -387,13 +392,15 @@ def tile_smoothed_square_scores_h1_kernel(
                 fit(c + 2, 0)
                 fit(c + 2, 1)
             if more:
-                round_on_scalar(left, 0, HALF - GPSIMD_COLS)
-                round_on_scalar(right, GPSIMD_COLS, HALF)
+                round_on_scalar(left, LEFT_VECTOR_COLS, HALF - GPSIMD_COLS)
+                round_on_scalar(right, GPSIMD_COLS, HALF - RIGHT_VECTOR_COLS)
                 apply_sign(c + 1, whole, range(PACK))
+                round_on_vector(left, 0, LEFT_VECTOR_COLS)
                 for half in range(2):
                     interleave_z(c + 1, half)
                 for half in range(2):
                     quantise_z(c + 1, half)
+                round_on_vector(right, HALF - RIGHT_VECTOR_COLS, HALF)
                 quantise_y(left)
             if c + 2 < GROUPS:
                 square(c + 2, 0, whole)
@@ -403,9 +410,9 @@ def tile_smoothed_square_scores_h1_kernel(
         for u in range(PACK):
             score(final, u)
             root(final, u)
-        round_on_vector(left, HALF - GPSIMD_COLS)
+        round_on_vector(left, 0, HALF - GPSIMD_COLS)
         for unit, cols in zip((right, final), TAIL_VECTOR_COLS):
-            round_on_vector(unit, cols)
+            round_on_vector(unit, 0, cols)
             round_on_scalar(unit, cols, HALF // 2)
             if unit == right:
                 quantise_y(left)

@@ -22,9 +22,9 @@ KP = P * PACK
 GROUPS = OBS // KP
 HALF = COMP // 2
 GPSIMD_COLS = 288
-LEFT_VECTOR_COLS = 112
-RIGHT_VECTOR_COLS = 0
-TAIL_VECTOR_COLS = (128, 160)
+LEFT_VECTOR_COLS = 48
+Z_SCALAR_COLS = 64
+TAIL_VECTOR_COLS = (64, 128)
 SQRT_MIN = 2.0 ** -116
 
 
@@ -51,14 +51,12 @@ def tile_smoothed_square_scores_h1_kernel(
         gain_sb = kept("gain_sb", [P, PACK], BF16)
         floor_sb = kept("floor_sb", [P, COMP // P], BF16)
         nc.scalar.dma_start(out=gain_sb[:], in_=gain.rearrange("(p t) -> p t", t=PACK))
-        nc.gpsimd.dma_start(out=floor_sb[:], in_=floor.rearrange("(p c) -> p c", p=P))
 
         cw_sb = kept("cw_sb", [P, GROUPS, 16], BF16)
-        nc.gpsimd.dma_start(out=cw_sb[:, :, 0:PACK], in_=case_weight.rearrange("(g p t) -> p g t", p=P, t=PACK))
 
-        s_plane = [kept("s_plane%d" % i, [P, GROUPS, 2 * KP], U8) for i in range(2)]
+        s_plane = [kept("s_plane%d" % i, [P, GROUPS, width * KP], U8) for i, width in enumerate((1, 1, 2))]
         w_plane = kept("w_plane", [P, 1, COMP], U8)
-        for plane in (s_plane[0], w_plane, s_plane[1]):
+        for plane in (s_plane[0], s_plane[1], w_plane, s_plane[2]):
             nc.vector.memset(plane[:].bitcast(I32), 0)
 
         r_raw = {}
@@ -80,23 +78,27 @@ def tile_smoothed_square_scores_h1_kernel(
                 s_sb[c, g] = words[:, g - first, :]
 
         load_responses(0)
-        load_scale_rows(nc.sync, s_plane[0], s_scales[:, :, 0 : 2 * KP])
+        load_scale_rows(nc.sync, s_plane[0], s_scales[:, :, 0:KP])
         load_s(0, 0, 2)
         load_responses(1)
         load_responses(2)
         load_s(0, 2, 3)
         load_responses(3)
         load_s(0, 3, 4)
+        nc.sync.dma_start(out=floor_sb[:], in_=floor.rearrange("(p c) -> p c", p=P))
+        load_s(1, 0, GROUPS)
+        load_scale_rows(nc.sync, s_plane[1], s_scales[:, :, KP : 2 * KP])
+        nc.sync.dma_start(out=cw_sb[:, :, 0:PACK], in_=case_weight.rearrange("(g p t) -> p g t", p=P, t=PACK))
         w_sb = kept("w_sb", [P, 2 * COMP], U8)
         nc.sync.dma_start(out=w_sb[:].bitcast(I32), in_=w_words[0].bitcast(I32))
         load_scale_rows(nc.sync, w_plane, w_scales)
-        load_s(1, 0, GROUPS)
         load_s(2, 0, GROUPS)
-        load_scale_rows(nc.sync, s_plane[1], s_scales[:, :, 2 * KP :])
+        load_scale_rows(nc.sync, s_plane[2], s_scales[:, :, 2 * KP :])
         load_s(3, 0, GROUPS)
 
         def s_operand(c, g):
-            return s_sb[c, g], s_plane[c // 2][:, g, (c % 2) * KP : (c % 2 + 1) * KP]
+            first = max(c - 2, 0) * KP
+            return s_sb[c, g], s_plane[min(c, 2)][:, g, first : first + KP]
 
         ident = kept("ident", [P, P], BF16)
         make_identity(nc, ident[:])
@@ -128,7 +130,6 @@ def tile_smoothed_square_scores_h1_kernel(
             lambda: nc.vector.scalar_tensor_tensor(
                 out=g_root[:], in0=g_guess[:], scalar=0.5, in1=g_corr[:], op0=ALU.mult, op1=ALU.add
             ),
-            lambda: nc.vector.tensor_tensor(out=cw_sq[:], in0=cw_sb[:, :, 0:PACK], in1=cw_sb[:, :, 0:PACK], op=ALU.mult),
         ]
 
         r_codes = {}
@@ -183,7 +184,8 @@ def tile_smoothed_square_scores_h1_kernel(
         for g in range(GROUPS):
             lower = interleave_responses(g, 0)
             upper = interleave_responses(g, 1)
-            newton[g]()
+            if g < len(newton):
+                newton[g]()
             if waiting is not None:
                 finish_upper(g - 1, waiting)
             quantise_responses(g, 0, lower)
@@ -229,14 +231,17 @@ def tile_smoothed_square_scores_h1_kernel(
                 row = z_sq[c, piece][:, s, :]
                 nc.vector.tensor_scalar(out=row, in0=row, scalar1=g_sign[:, s : s + 1], scalar2=None, op0=ALU.mult)
 
-        def interleave_z(c, half):
+        def interleave_z(c, half, on_scalar):
             piece = [pc for pc in pieces(c) if pc[0] <= 2 * half < pc[1]][0]
             first = (2 * half - piece[0]) * P
             grouped = work.tile([P, 2 * P, PACK], BF16, name="z_grouped", tag="z_grouped", align_bytes=64)
-            nc.vector.tensor_copy(
-                out=grouped[:].rearrange("p (a i) s -> p a s i", i=4),
-                in_=z_sq[c, piece][:, :, first : first + 2 * P].rearrange("p s (a i) -> p a s i", i=4),
-            )
+            dst = grouped[:].rearrange("p (a i) s -> p a s i", i=4)
+            src = z_sq[c, piece][:, :, first : first + 2 * P].rearrange("p s (a i) -> p a s i", i=4)
+            cut = (2 * P - on_scalar) // 4
+            if cut > 0:
+                nc.vector.tensor_copy(out=dst[:, 0:cut], in_=src[:, 0:cut])
+            if on_scalar:
+                nc.scalar.copy(out=dst[:, cut:], in_=src[:, cut:])
             z_grouped[c, half] = grouped
 
         def quantise_z(c, half):
@@ -307,14 +312,12 @@ def tile_smoothed_square_scores_h1_kernel(
             )
 
         def round_on_vector(unit, first, end):
-            if end > first:
-                dst, src = round_views(unit, first, end)
-                nc.vector.tensor_copy(out=dst, in_=src)
+            dst, src = round_views(unit, first, end)
+            nc.vector.tensor_copy(out=dst, in_=src)
 
         def round_on_scalar(unit, first, end):
-            nc.scalar.copy(
-                out=grouped_view(unit)[:, first:end, :], in_=y[unit][:, :, first:end].rearrange("p t n -> p n t")
-            )
+            dst, src = round_views(unit, first, end)
+            nc.scalar.copy(out=dst, in_=src)
 
         y_codes = {}
 
@@ -344,7 +347,7 @@ def tile_smoothed_square_scores_h1_kernel(
         copy_floor(0)
         fit(1, 0)
         apply_sign(0, (0, 2), range(PACK))
-        interleave_z(0, 0)
+        interleave_z(0, 0, 0)
         apply_sign(0, (2, 4), range(PACK - 1))
         quantise_z(0, 0)
         score(units[0], 0)
@@ -353,7 +356,8 @@ def tile_smoothed_square_scores_h1_kernel(
         copy_floor(1)
         fit(1, 1)
         apply_sign(0, (2, 4), [PACK - 1])
-        interleave_z(0, 1)
+        nc.vector.tensor_tensor(out=cw_sq[:], in0=cw_sb[:, :, 0:PACK], in1=cw_sb[:, :, 0:PACK], op=ALU.mult)
+        interleave_z(0, 1, 0)
         root(units[0], 0)
         quantise_z(0, 1)
         score(units[0], 2)
@@ -392,15 +396,14 @@ def tile_smoothed_square_scores_h1_kernel(
                 fit(c + 2, 0)
                 fit(c + 2, 1)
             if more:
-                round_on_scalar(left, LEFT_VECTOR_COLS, HALF - GPSIMD_COLS)
-                round_on_scalar(right, GPSIMD_COLS, HALF - RIGHT_VECTOR_COLS)
                 apply_sign(c + 1, whole, range(PACK))
                 round_on_vector(left, 0, LEFT_VECTOR_COLS)
-                for half in range(2):
-                    interleave_z(c + 1, half)
+                interleave_z(c + 1, 0, 0)
+                interleave_z(c + 1, 1, Z_SCALAR_COLS)
+                round_on_scalar(left, LEFT_VECTOR_COLS, HALF - GPSIMD_COLS)
+                round_on_scalar(right, GPSIMD_COLS, HALF)
                 for half in range(2):
                     quantise_z(c + 1, half)
-                round_on_vector(right, HALF - RIGHT_VECTOR_COLS, HALF)
                 quantise_y(left)
             if c + 2 < GROUPS:
                 square(c + 2, 0, whole)

from contextlib import ExitStack

import concourse.mybir as mybir
from concourse.masks import make_identity

OBS, OUTC, COMP = 2048, 512, 1024
FLOPS = 2 * OBS * OBS * OUTC + 2 * OBS * OUTC * COMP

F32 = mybir.dt.float32
BF16 = mybir.dt.bfloat16
I32 = mybir.dt.int32
U32 = mybir.dt.uint32
U8 = mybir.dt.uint8
FP8X4 = mybir.dt.float8_e4m3fn_x4
FP4X4 = mybir.dt.float4_e2m1fn_x4
ALU = mybir.AluOpType
ACT = mybir.ActivationFunctionType

P = 128
PACK = 4
KP = P * PACK
GROUPS = OBS // KP
HALF = COMP // 2
GPSIMD_COLS = 288
LEFT_VECTOR_COLS = 48
Z_SCALAR_COLS = 64
TAIL_VECTOR_COLS = (64, 128)
SQRT_MIN = 2.0 ** -116


def tile_smoothed_square_scores_h1_kernel(
    tc, s_words, s_scales, responses, gain, w_words, w_scales, floor, case_weight, out_0, out_1, out_2
):
    nc = tc.nc
    with ExitStack() as ctx:
        keep = ctx.enter_context(tc.tile_pool(name="keep", bufs=1))
        work = ctx.enter_context(tc.tile_pool(name="work", bufs=2))
        psum = ctx.enter_context(tc.psum_pool(name="psum", bufs=1))
        ctx.enter_context(tc.manual_schedule())

        def kept(name, shape, dtype):
            return keep.tile(shape, dtype, name=name, tag=name, align_bytes=64)

        def load_scale_rows(queue, plane, rows):
            for q in range(4):
                queue.dma_start(
                    out=plane[32 * q : 32 * q + 4, :, :].bitcast(I32),
                    in_=rows[:, 4 * q : 4 * q + 4, :].rearrange("g r n -> r g n").bitcast(I32),
                )

        gain_sb = kept("gain_sb", [P, PACK], BF16)
        floor_sb = kept("floor_sb", [P, COMP // P], BF16)
        nc.scalar.dma_start(out=gain_sb[:], in_=gain.rearrange("(p t) -> p t", t=PACK))

        cw_sb = kept("cw_sb", [P, GROUPS, 16], BF16)

        s_plane = [kept("s_plane%d" % i, [P, GROUPS, width * KP], U8) for i, width in enumerate((1, 1, 2))]
        w_plane = kept("w_plane", [P, 1, COMP], U8)
        for plane in (s_plane[0], s_plane[1], w_plane, s_plane[2]):
            nc.vector.memset(plane[:].bitcast(I32), 0)

        r_raw = {}
        s_sb = {}

        def load_responses(g):
            r_raw[g] = kept("r_raw%d" % g, [P, PACK, OUTC], BF16)
            nc.sync.dma_start(
                out=r_raw[g][:], in_=responses[g * KP : (g + 1) * KP, :].rearrange("(p j) o -> p j o", j=PACK)
            )

        def load_s(c, first, end):
            words = kept("s_sb%d_%d" % (c, first), [P, end - first, 2 * KP], U8)
            nc.sync.dma_start(
                out=words[:].bitcast(I32),
                in_=s_words[first:end, :, 2 * KP * c : 2 * KP * (c + 1)].rearrange("g p n -> p g n").bitcast(I32),
            )
            for g in range(first, end):
                s_sb[c, g] = words[:, g - first, :]

        load_responses(0)
        load_scale_rows(nc.sync, s_plane[0], s_scales[:, :, 0:KP])
        load_s(0, 0, 2)
        load_responses(1)
        load_responses(2)
        load_s(0, 2, 3)
        load_responses(3)
        load_s(0, 3, 4)
        nc.sync.dma_start(out=floor_sb[:], in_=floor.rearrange("(p c) -> p c", p=P))
        load_s(1, 0, GROUPS)
        load_scale_rows(nc.sync, s_plane[1], s_scales[:, :, KP : 2 * KP])
        nc.sync.dma_start(out=cw_sb[:, :, 0:PACK], in_=case_weight.rearrange("(g p t) -> p g t", p=P, t=PACK))
        w_sb = kept("w_sb", [P, 2 * COMP], U8)
        nc.sync.dma_start(out=w_sb[:].bitcast(I32), in_=w_words[0].bitcast(I32))
        load_scale_rows(nc.sync, w_plane, w_scales)
        load_s(2, 0, GROUPS)
        load_scale_rows(nc.sync, s_plane[2], s_scales[:, :, 2 * KP :])
        load_s(3, 0, GROUPS)

        def s_operand(c, g):
            first = max(c - 2, 0) * KP
            return s_sb[c, g], s_plane[min(c, 2)][:, g, first : first + KP]

        ident = kept("ident", [P, P], BF16)
        make_identity(nc, ident[:])
        floor_ps = psum.tile([P, COMP // P, P], BF16, name="floor_ps", tag="score3")

        g_neg = kept("g_neg", [P, PACK], F32)
        g_abs = kept("g_abs", [P, PACK], F32)
        g_guess = kept("g_guess", [P, PACK], F32)
        g_recip = kept("g_recip", [P, PACK], F32)
        g_corr = kept("g_corr", [P, PACK], F32)
        g_root = kept("g_root", [P, PACK], F32)
        g_below = kept("g_below", [P, PACK], F32)
        g_sign = kept("g_sign", [P, PACK], F32)
        nc.vector.tensor_scalar(out=g_neg[:], in0=gain_sb[:], scalar1=-1.0, scalar2=None, op0=ALU.mult)
        nc.vector.tensor_scalar(out=g_below[:], in0=gain_sb[:], scalar1=0.0, scalar2=None, op0=ALU.is_lt)
        nc.vector.scalar_tensor_tensor(
            out=g_abs[:], in0=gain_sb[:], scalar=SQRT_MIN, in1=g_neg[:], op0=ALU.max, op1=ALU.max
        )
        nc.vector.scalar_tensor_tensor(
            out=g_sign[:], in0=gain_sb[:], scalar=0.0, in1=g_below[:], op0=ALU.is_gt, op1=ALU.subtract
        )
        nc.scalar.activation(out=g_guess[:], in_=g_abs[:], func=ACT.Sqrt)
        cw_sq = kept("cw_sq", [P, GROUPS, PACK], F32)
        newton = [
            lambda: nc.vector.reciprocal(out=g_recip[:], in_=g_guess[:]),
            lambda: nc.vector.scalar_tensor_tensor(
                out=g_corr[:], in0=g_abs[:], scalar=0.5, in1=g_recip[:], op0=ALU.mult, op1=ALU.mult
            ),
            lambda: nc.vector.scalar_tensor_tensor(
                out=g_root[:], in0=g_guess[:], scalar=0.5, in1=g_corr[:], op0=ALU.mult, op1=ALU.add
            ),
        ]

        r_codes = {}
        r_scales = {}

        def interleave_responses(g, part):
            grouped = work.tile([P, 2, P, PACK], BF16, name="r_grouped", tag="r_grouped%d" % part, align_bytes=64)
            dst = grouped[:].rearrange("p s (a b) j -> p a s b j", b=2)
            src = r_raw[g][:].rearrange("p j (a b s) -> p a s b j", b=2, s=PACK)[:, :, 2 * part : 2 * part + 2, :, :]
            if part == 0:
                nc.vector.tensor_copy(out=dst, in_=src)
            else:
                nc.scalar.copy(out=dst, in_=src)
            return grouped

        def quantise_responses(g, part, grouped):
            codes = kept("r_codes%d_%d" % (g, part), [P, 2 * P], U32)
            scales = kept("r_scales%d_%d" % (g, part), [P, 2 * P], U8)
            nc.vector.quantize_mx(
                out=codes[:].bitcast(FP8X4), scales=scales[:], in_=grouped[:].rearrange("p s m j -> p (s m j)")
            )
            r_codes[g, part] = codes
            r_scales[g, part] = scales

        fit_ps = {}

        def fit_pass(c, s, g):
            if g == 0:
                fit_ps[c, s] = psum.tile([P, KP], F32, name="fit_ps", tag="fit%d" % s)
            words, plane = s_operand(c, g)
            cols = slice((s % 2) * P, (s % 2 + 1) * P)
            nc.tensor.matmul_mx(
                out=fit_ps[c, s][:],
                lhsT=r_codes[g, s // 2][:, cols].bitcast(FP8X4),
                lhsT_scale=r_scales[g, s // 2][:, cols],
                rhs=words.bitcast(FP4X4),
                rhs_scale=plane,
                start=(g == 0),
                stop=(g == GROUPS - 1),
            )

        def fit(c, s):
            for g in range(GROUPS):
                fit_pass(c, s, g)

        def finish_upper(g, grouped):
            quantise_responses(g, 1, grouped)
            fit_pass(0, 2, g)
            fit_pass(0, 3, g)

        waiting = None
        for g in range(GROUPS):
            lower = interleave_responses(g, 0)
            upper = interleave_responses(g, 1)
            if g < len(newton):
                newton[g]()
            if waiting is not None:
                finish_upper(g - 1, waiting)
            quantise_responses(g, 0, lower)
            fit_pass(0, 0, g)
            fit_pass(0, 1, g)
            waiting = upper
            if g in (0, GROUPS - 1):
                finish_upper(g, upper)
                waiting = None

        for c in range(COMP // P):
            nc.tensor.transpose(floor_ps[:, c, :], floor_sb[:, c : c + 1].to_broadcast([P, P]), ident[:])

        floor_all = [kept("floor_all%d" % h, [P, HALF], F32) for h in range(2)]

        def copy_floor(h):
            nc.scalar.copy(
                out=floor_all[h][:].rearrange("p (n c) -> p n c", c=COMP // P),
                in_=floor_ps[:, :, h * P // 2 : (h + 1) * P // 2].rearrange("p c n -> p n c"),
            )

        z_sq = {}
        z_grouped = {}
        z_codes = {}
        z_scales = {}

        def pieces(c):
            return [(0, 2), (2, 4)] if c == 0 else [(0, 4)]

        def square(c, s, piece):
            lo, hi = piece
            if s == 0:
                z_sq[c, piece] = work.tile([P, PACK, (hi - lo) * P], BF16, name="z_sq", tag="z_sq", bufs=3, align_bytes=64)
            nc.scalar.activation(
                out=z_sq[c, piece][:, s, :].rearrange("p (u m) -> p u m", m=P),
                in_=fit_ps[c, s][:].rearrange("p (m u) -> p u m", u=PACK)[:, lo:hi, :],
                func=ACT.Square,
                scale=g_root[:, s : s + 1],
            )

        def apply_sign(c, piece, slots):
            for s in slots:
                row = z_sq[c, piece][:, s, :]
                nc.vector.tensor_scalar(out=row, in0=row, scalar1=g_sign[:, s : s + 1], scalar2=None, op0=ALU.mult)

        def interleave_z(c, half, on_scalar):
            piece = [pc for pc in pieces(c) if pc[0] <= 2 * half < pc[1]][0]
            first = (2 * half - piece[0]) * P
            grouped = work.tile([P, 2 * P, PACK], BF16, name="z_grouped", tag="z_grouped", align_bytes=64)
            dst = grouped[:].rearrange("p (a i) s -> p a s i", i=4)
            src = z_sq[c, piece][:, :, first : first + 2 * P].rearrange("p s (a i) -> p a s i", i=4)
            cut = (2 * P - on_scalar) // 4
            if cut > 0:
                nc.vector.tensor_copy(out=dst[:, 0:cut], in_=src[:, 0:cut])
            if on_scalar:
                nc.scalar.copy(out=dst[:, cut:], in_=src[:, cut:])
            z_grouped[c, half] = grouped

        def quantise_z(c, half):
            codes = work.tile([P, 2 * P], U32, name="z_codes", tag="z_codes", bufs=4, align_bytes=64)
            scales = work.tile([P, 2 * P], U8, name="z_scales", tag="z_scales", bufs=4, align_bytes=64)
            nc.vector.quantize_mx(
                out=codes[:].bitcast(FP8X4), scales=scales[:], in_=z_grouped[c, half][:].rearrange("p n s -> p (n s)")
            )
            z_codes[c, half] = codes
            z_scales[c, half] = scales

        score_ps = {}
        y = {}
        y_grouped = {}
        y_plane = kept("y_plane", [P, COMP], U8)

        def score(unit, u):
            c, lo, hi = unit
            bank = psum.tile([P, hi - lo], F32, name="score_ps", tag="score%d" % u)
            cols = slice((u % 2) * P, (u % 2 + 1) * P)
            nc.tensor.matmul_mx(
                out=bank[:],
                lhsT=z_codes[c, u // 2][:, cols].bitcast(FP8X4),
                lhsT_scale=z_scales[c, u // 2][:, cols],
                rhs=w_sb[:, 2 * lo : 2 * hi].bitcast(FP4X4),
                rhs_scale=w_plane[:, 0, lo:hi],
                start=True,
                stop=True,
            )
            score_ps[unit, u] = bank

        def root(unit, u):
            c, lo, hi = unit
            raised = work.tile([P, hi - lo], F32, name="raised", tag="raised", bufs=6, align_bytes=64)
            nc.vector.tensor_tensor(out=raised[:], in0=score_ps[unit, u][:], in1=floor_all[lo // HALF][:, lo % HALF : lo % HALF + hi - lo], op=ALU.add)
            if u == 0:
                y[unit] = work.tile([P, PACK, hi - lo], F32, name="y", tag="y", bufs=3, align_bytes=64)
            nc.scalar.activation(out=y[unit][:, u, :], in_=raised[:], func=ACT.Sqrt, scale=cw_sq[:, c, u : u + 1])
            run = PACK if unit in units[-2:] else 2
            if (u + 1) % run == 0:
                rows = out_0[c * KP : (c + 1) * KP, lo:hi].rearrange("(p t) n -> p t n", t=PACK)
                nc.sync.dma_start(out=rows[:, u + 1 - run : u + 1, :], in_=y[unit][:, u + 1 - run : u + 1, :])

        shared = kept("y_shared", [P, 2 * HALF - GPSIMD_COLS, PACK], BF16)

        def grouped_view(unit):
            if unit in units[-2:]:
                if unit not in y_grouped:
                    y_grouped[unit] = work.tile([P, HALF // 2, PACK], BF16, name="y_tail", tag="y_tail", align_bytes=64)
                return y_grouped[unit][:]
            start = 0 if unit[1] == 0 else HALF - GPSIMD_COLS
            return shared[:, start : start + HALF, :]

        def round_views(unit, first, end):
            dst = grouped_view(unit)[:, first:end, :].rearrange("p (a i) t -> p a t i", i=4)
            src = y[unit][:, :, first:end].rearrange("p t (a i) -> p a t i", i=4)
            return dst, src

        def round_on_gpsimd(unit):
            first = HALF - GPSIMD_COLS if unit[1] == 0 else 0
            nc.gpsimd.tensor_scalar(
                out=grouped_view(unit)[:, first : first + GPSIMD_COLS, :],
                in0=y[unit][:, :, first : first + GPSIMD_COLS].rearrange("p t n -> p n t"),
                scalar1=1.0,
                scalar2=0.0,
                op0=ALU.mult,
                op1=ALU.add,
            )

        def round_on_vector(unit, first, end):
            dst, src = round_views(unit, first, end)
            nc.vector.tensor_copy(out=dst, in_=src)

        def round_on_scalar(unit, first, end):
            dst, src = round_views(unit, first, end)
            nc.scalar.copy(out=dst, in_=src)

        y_codes = {}

        def quantise_y(unit):
            c, lo, hi = unit
            start = lo - lo % HALF
            if lo == start:
                y_codes[c, start] = work.tile([P, HALF], U32, name="y_codes", tag="y_codes", bufs=3, align_bytes=64)
            codes = y_codes[c, start]
            nc.vector.quantize_mx(
                out=codes[:, lo - start : hi - start].bitcast(FP8X4),
                scales=y_plane[PACK * c : P, lo:hi],
                in_=grouped_view(unit).rearrange("p n t -> p (n t)"),
            )
            if hi == start + HALF:
                words = out_1[c].rearrange("p n t -> p (n t)")[:, PACK * start : PACK * hi]
                nc.sync.dma_start(out=words.bitcast(I32), in_=codes[:].bitcast(I32))

        whole = (0, PACK)
        last = GROUPS - 1
        units = [(c, HALF * h, HALF * (h + 1)) for c in range(GROUPS) for h in range(2)][:-1]
        units = units + [(last, HALF, HALF + HALF // 2), (last, HALF + HALF // 2, COMP)]

        for piece in pieces(0):
            for s in range(PACK):
                square(0, s, piece)
        copy_floor(0)
        fit(1, 0)
        apply_sign(0, (0, 2), range(PACK))
        interleave_z(0, 0, 0)
        apply_sign(0, (2, 4), range(PACK - 1))
        quantise_z(0, 0)
        score(units[0], 0)
        score(units[0], 1)
        square(1, 0, whole)
        copy_floor(1)
        fit(1, 1)
        apply_sign(0, (2, 4), [PACK - 1])
        nc.vector.tensor_tensor(out=cw_sq[:], in0=cw_sb[:, :, 0:PACK], in1=cw_sb[:, :, 0:PACK], op=ALU.mult)
        interleave_z(0, 1, 0)
        root(units[0], 0)
        quantise_z(0, 1)
        score(units[0], 2)
        score(units[0], 3)
        square(1, 1, whole)

        for c in range(GROUPS):
            more = c + 1 < GROUPS
            left, right = units[2 * c], units[2 * c + 1]
            if c > 0:
                before = units[2 * c - 1]
                round_on_gpsimd(before)
                for u in range(PACK):
                    score(left, u)
            if more and c > 0:
                fit(c + 1, 2)
            for u in range(1 if c == 0 else 0, PACK):
                root(left, u)
            if c > 0:
                quantise_y(before)
            for u in range(PACK):
                score(right, u)
                if c == 0 and u == 1:
                    fit(1, 2)
            round_on_gpsimd(left)
            if more:
                square(c + 1, 2, whole)
                fit(c + 1, 3)
            root(right, 0)
            root(right, 1)
            if more:
                square(c + 1, 3, whole)
            root(right, 2)
            root(right, 3)
            if c + 2 < GROUPS:
                fit(c + 2, 0)
                fit(c + 2, 1)
            if more:
                apply_sign(c + 1, whole, range(PACK))
                round_on_vector(left, 0, LEFT_VECTOR_COLS)
                interleave_z(c + 1, 0, 0)
                interleave_z(c + 1, 1, Z_SCALAR_COLS)
                round_on_scalar(left, LEFT_VECTOR_COLS, HALF - GPSIMD_COLS)
                round_on_scalar(right, GPSIMD_COLS, HALF)
                for half in range(2):
                    quantise_z(c + 1, half)
                quantise_y(left)
            if c + 2 < GROUPS:
                square(c + 2, 0, whole)
                square(c + 2, 1, whole)

        left, right, final = units[-3:]
        for u in range(PACK):
            score(final, u)
            root(final, u)
        round_on_vector(left, 0, HALF - GPSIMD_COLS)
        for unit, cols in zip((right, final), TAIL_VECTOR_COLS):
            round_on_vector(unit, 0, cols)
            round_on_scalar(unit, cols, HALF // 2)
            if unit == right:
                quantise_y(left)
        quantise_y(right)
        quantise_y(final)
        for q in range(4):
            nc.scalar.dma_start(
                out=out_2[:, 4 * q : 4 * q + 4, :].bitcast(I32),
                in_=y_plane[32 * q : 32 * q + 16, :].bitcast(I32),
            )
